import numpy as np
import ml_dtypes


def mxq(x, axis, fmt="e4m3"):
    dtype, down = {"e4m3": (ml_dtypes.float8_e4m3fn, 7), "e5m2": (ml_dtypes.float8_e5m2, 14)}[fmt]
    v = np.moveaxis(np.asarray(x, np.float32).astype(ml_dtypes.bfloat16).astype(np.float64), axis, -1)
    blocks = v.reshape(v.shape[:-1] + (-1, 32))
    amax = np.abs(blocks).max(-1, keepdims=True)
    byte = np.maximum(np.where(amax > 0, np.frexp(amax)[1] - 1 + 127, 0) - down, 1)
    scale = np.exp2(byte - 127.0)
    codes = (blocks / scale).astype(np.float32).astype(dtype).astype(np.float64)
    return np.moveaxis((codes * scale).reshape(v.shape), -1, axis)


WIDE = False


def mx_kscale(k, group=512):
    if not WIDE:
        return np.ones(k)
    levels = np.array([10, -10, 5, -5, 0])
    if group != 512:
        return np.exp2(np.random.permutation(np.resize(levels, k // group))).repeat(group)
    if k % 512:
        return np.exp2(np.random.permutation(np.resize(levels, k // 32))).repeat(32)
    a = np.empty((k // 512, 16))
    for p in range(k // 512):
        a[p, :8] = np.random.permutation(np.resize(levels, 8))
        for g in range(8):
            far = levels[np.abs(levels - a[p, g]) >= 10]
            a[p, g + 8] = far[np.random.randint(len(far))]
    return np.exp2(a.ravel()).repeat(32)


def f64(x):
    return np.asarray(x).astype(np.float64)


def striped(idx):
    return np.tile(np.asarray(idx).reshape(-1, 16).T, (8, 1)).astype(np.uint16)


def unstriped(offs):
    return offs[:16].T.reshape(-1).astype(np.int64)


H, KV, D, NQ, N = 4, 1, 256, 512, 512


def setup_inputs():
    n = np.random.standard_normal
    s = mx_kscale(D, 0)[:, None]
    u = mx_kscale(N)
    t = np.random.uniform(0.5, 2.0, N) * u
    v = n((KV, N, 128))
    return {
        "qT": (n((H, D, NQ)) * s * (0.70 / np.sqrt(D))).astype(np.float32),
        "kT": (n((KV, D, N)) / s).astype(np.float32),
        "t": t.reshape(N, 1).astype(np.float32),
        "v": (v / t[:, None]).astype(np.float32),
        "kb": (0.5 * n((N, 1))).astype(np.float32),
        "gn": np.tile(np.random.uniform(0.5, 2.0, 128), (128, 1)).astype(np.float32),
        "og": n((H, NQ, 128)).astype(np.float32),
    }


def reference(qT, kT, t, v, kb, gn, og):
    a = np.repeat(mxq(f64(kT), 1, "e4m3"), H // KV, 0).transpose(0, 2, 1) @ mxq(f64(qT), 1, "e4m3")
    a = a + f64(kb)
    p = a / (1.0 + np.exp(-a))
    w = p * f64(t)
    y = mxq(w, 1, "e4m3").transpose(0, 2, 1) @ np.repeat(mxq(f64(v), 1, "e4m3"), H // KV, 0)
    y = y / 16.0
    y = y / np.sqrt(np.mean(np.square(y), -1, keepdims=True) + 1e-5) * f64(gn)[:1]
    y = y / (1.0 + np.exp(-f64(og)))
    return y

@@ -1,0 +1,386 @@
+from contextlib import ExitStack
+
+import concourse.mybir as mybir
+
+H, D, NQ, N, E = 4, 256, 512, 512, 128
+FLOPS = 2 * H * N * NQ * (D + E)
+
+F32 = mybir.dt.float32
+BF16 = mybir.dt.bfloat16
+U32 = mybir.dt.uint32
+I32 = mybir.dt.int32
+U8 = mybir.dt.uint8
+FP8X4 = mybir.dt.float8_e4m3fn_x4
+ACT = mybir.ActivationFunctionType
+ALU = mybir.AluOpType
+
+P = 128
+R = 64
+PACK = 4
+T = 128
+RUN = 4
+BANK = 512
+DEAL = (1, 2, 2, 2)
+
+
+def tile_rows_a_silu_kb_onorm_gate_kernel(tc, qT, kT, t, v, kb, gn, og, out):
+    nc = tc.nc
+    with ExitStack() as ctx:
+        keep = ctx.enter_context(tc.tile_pool(name="keep", bufs=1))
+        psum = ctx.enter_context(tc.psum_pool(name="psum", bufs=2))
+        ctx.enter_context(tc.manual_schedule())
+
+        q_rows = qT.rearrange("h d n -> (h d) n")
+        k_rows = kT[0].rearrange("(p j) n -> p j n", j=PACK)
+
+        kb_sb = keep.tile([P, PACK], F32, name="kb_sb")
+        t_sb = keep.tile([P, PACK], F32, name="t_sb")
+        gn_sb = keep.tile([P, E], F32, name="gn_sb")
+        v_raw = keep.tile([P, PACK, E], F32, name="v_raw")
+        v_bf = keep.tile([P, E, PACK], BF16, name="v_bf", align_bytes=64)
+        v_codes = keep.tile([P, E], U32, name="v_codes", align_bytes=64)
+        v_scales = keep.tile([P, E], U8, name="v_scales", align_bytes=64)
+        k_bf = keep.tile([R, PACK, T, PACK], BF16, name="k_bf", align_bytes=64)
+        k_mx = [keep.tile([P, N + N // 4], U32, name="k_mx%d" % g, align_bytes=64) for g in range(2)]
+        warm = keep.tile([P, 2], F32, name="warm")
+        sumsq = keep.tile([P, H * PACK], F32, name="sumsq")
+        squares = keep.tile([P, H * PACK, E], F32, name="squares")
+        y_ps = [psum.tile([P, BANK], F32, name="y%d" % h, bufs=1) for h in range(H)]
+
+        k_raw, q_raw, q_bf, q_mx, og_sb, gate = {}, {}, {}, {}, {}, {}
+        banks, probs, w_bf, w_mx, rstd = {}, {}, {}, {}, {}
+
+        def by_tile(rows, h):
+            deal = DEAL[h]
+            return rows.rearrange("(u s i) e -> s u (i e)", s=P, i=deal)
+
+
+        def load_k(c0, c1):
+            k_raw[c0] = keep.tile([R, PACK, c1 - c0], F32, name="k_raw%d" % c0)
+            nc.sync.dma_start(out=k_raw[c0][:], in_=k_rows[:, :, c0:c1])
+
+        def load_q(pair, c0, c1, queue=nc.sync):
+            q_raw[pair, c0] = keep.tile([P, PACK, c1 - c0], F32, name="q_raw%d_%d" % (pair, c0))
+            rows = q_rows[2 * D * pair : 2 * D * (pair + 1), :].rearrange("(p j) n -> p j n", j=PACK)
+            queue.dma_start(out=q_raw[pair, c0][:], in_=rows[:, :, c0:c1])
+
+        def load_v():
+            nc.sync.dma_start(out=v_raw[:], in_=v[0].rearrange("(p j) e -> p j e", j=PACK))
+
+        def load_gn():
+            nc.sync.dma_start(out=gn_sb[:], in_=gn)
+
+        def load_og(h):
+            og_sb[h] = keep.tile([P, NQ // T, E], F32, name="og%d" % h)
+            nc.sync.dma_start(out=og_sb[h][:].rearrange("p (u i) e -> p u (i e)", i=DEAL[h]), in_=by_tile(og[h], h))
+
+        def copy_on(engine, dst, src):
+            if engine == "vector":
+                nc.vector.tensor_copy(out=dst, in_=src)
+            else:
+                nc.scalar.copy(out=dst, in_=src)
+
+        def round_k(c0, c1, engine):
+            copy_on(
+                engine,
+                k_bf[:, :, c0 // PACK : c1 // PACK, :].rearrange("p r s j -> p s j r"),
+                k_raw[c0][:].rearrange("p j (s r) -> p s j r", r=PACK),
+            )
+
+        def k_operand(g, r):
+            rows = slice(R * g, R * (g + 1))
+            codes = k_mx[g][rows, T * r : T * (r + 1)].bitcast(FP8X4)
+            scales = k_mx[g][rows, N:].bitcast(U8)[:, T * r : T * (r + 1)]
+            return codes, scales
+
+        def quantize_k(r):
+            codes, scales = k_operand(0, r)
+            nc.vector.quantize_mx(out=codes, scales=scales, in_=k_bf[:, r, :, :].rearrange("p s j -> p (s j)"))
+
+        def move_k():
+            nc.sync.dma_start(out=k_mx[1][R:P, :].bitcast(I32), in_=k_mx[0][0:R, :].bitcast(I32))
+
+        def interleave(engine, dst, src):
+            copy_on(
+                engine,
+                dst.rearrange("p (c i) j -> p c j i", i=RUN),
+                src.rearrange("p j (c i) -> p c j i", i=RUN),
+            )
+
+        def round_q(pair, c0, engine):
+            width = q_raw[pair, c0].shape[2]
+            q_bf[pair, c0] = keep.tile([P, width, PACK], BF16, name="q_bf%d_%d" % (pair, c0), align_bytes=64)
+            interleave(engine, q_bf[pair, c0][:], q_raw[pair, c0][:])
+
+        def quantize_q(pair, c0):
+            width = q_raw[pair, c0].shape[2]
+            codes = keep.tile([P, width], U32, name="q_codes%d_%d" % (pair, c0), align_bytes=64)
+            scales = keep.tile([P, width], U8, name="q_scales%d_%d" % (pair, c0), align_bytes=64)
+            nc.vector.quantize_mx(
+                out=codes[:].bitcast(FP8X4), scales=scales[:], in_=q_bf[pair, c0][:].rearrange("p n j -> p (n j)")
+            )
+            for b in range(0, width, T):
+                q_mx[pair, c0 + b] = (codes, scales, b)
+
+        def round_v(engine):
+            interleave(engine, v_bf[:], v_raw[:])
+
+        def quantize_v():
+            nc.vector.quantize_mx(
+                out=v_codes[:].bitcast(FP8X4), scales=v_scales[:], in_=v_bf[:].rearrange("p e j -> p (e j)")
+            )
+
+        def scores(h, c0, c1, r0):
+            width = c1 - c0
+            g = h % 2
+            rows = slice(R * g, R * (g + 1))
+            bank = psum.tile([P, BANK], F32, name="s%d" % g, tag="s%d" % g)
+            banks[h, c0, r0] = bank
+            for r in range(r0, r0 + BANK // width):
+                k_codes, k_scales = k_operand(g, r)
+                for b in range(0, width, T):
+                    codes, scales, at = q_mx[h // 2, c0 + b]
+                    col = (r - r0) * width + b
+                    nc.tensor.matmul_mx(
+                        out=bank[:, col : col + T],
+                        lhsT=k_codes,
+                        lhsT_scale=k_scales,
+                        rhs=codes[rows, at : at + T].bitcast(FP8X4),
+                        rhs_scale=scales[rows, at : at + T],
+                        start=True,
+                        stop=True,
+                    )
+
+        def silu(h, c0, c1, r0):
+            width = c1 - c0
+            if r0 == 0:
+                probs[h, c0] = keep.tile([P, PACK, width], F32, name="probs%d_%d" % (h, c0))
+            for r in range(r0, r0 + BANK // width):
+                col = (r - r0) * width
+                nc.scalar.activation(
+                    out=probs[h, c0][:, r, :].rearrange("p (i s) -> p i s", i=DEAL[h]),
+                    in_=banks[h, c0, r0][:, col : col + width].rearrange("p (s i) -> p i s", i=DEAL[h]),
+                    func=ACT.Silu,
+                    bias=kb_sb[:, r : r + 1],
+                )
+
+        def weigh(h, c0, c1):
+            width = c1 - c0
+            w_bf[h, c0] = keep.tile([P, width, PACK], BF16, name="w%d_%d" % (h, c0), align_bytes=64)
+            nc.vector.tensor_tensor(
+                out=w_bf[h, c0][:].rearrange("p (c i) r -> p c r i", i=RUN),
+                in0=probs[h, c0][:].rearrange("p r (c i) -> p c r i", i=RUN),
+                in1=t_sb[:].unsqueeze(1).unsqueeze(3).broadcast_to([P, width // RUN, PACK, RUN]),
+                op=ALU.mult,
+            )
+
+        def quantize_w(h, c0, c1):
+            width = c1 - c0
+            codes = keep.tile([P, width], U32, name="w_codes%d_%d" % (h, c0), align_bytes=64)
+            scales = keep.tile([P, width], U8, name="w_scales%d_%d" % (h, c0), align_bytes=64)
+            nc.vector.quantize_mx(
+                out=codes[:].bitcast(FP8X4), scales=scales[:], in_=w_bf[h, c0][:].rearrange("p n r -> p (n r)")
+            )
+            w_mx[h, c0] = (codes, scales)
+
+        def values(h, c0, c1):
+            codes, scales = w_mx[h, c0]
+            for b in range(0, c1 - c0, T):
+                nc.tensor.matmul_mx(
+                    out=y_ps[h][:, c0 + b : c0 + b + E],
+                    lhsT=codes[:, b : b + T].bitcast(FP8X4),
+                    lhsT_scale=scales[:, b : b + T],
+                    rhs=v_codes[:].bitcast(FP8X4),
+                    rhs_scale=v_scales[:],
+                    start=True,
+                    stop=True,
+                )
+
+        def square(h, m):
+            col = PACK * h + m
+            nc.scalar.activation(
+                out=squares[:, col, :],
+                in_=y_ps[h][:, m * E : (m + 1) * E],
+                func=ACT.Square,
+                accum_out=sumsq[:, col : col + 1],
+            )
+
+        def inv_rms(c0, c1):
+            factor = keep.tile([P, c1 - c0], F32, name="factor%d" % c0)
+            nc.scalar.activation(
+                out=factor[:], in_=sumsq[:, c0:c1], func=ACT.Abs_reciprocal_sqrt, scale=1.0 / 32.0, bias=1024 * 1e-5
+            )
+            for c in range(c0, c1):
+                rstd[c] = factor[:, c - c0 : c - c0 + 1]
+
+        def gate_tanh(h):
+            nc.scalar.activation(out=og_sb[h][:], in_=og_sb[h][:], func=ACT.Tanh, scale=0.5)
+
+        def gate_gain(h):
+            gate[h] = keep.tile([P, NQ // T, E], F32, name="gate%d" % h)
+            nc.vector.scalar_tensor_tensor(
+                out=gate[h][:],
+                in0=og_sb[h][:],
+                scalar=1.0,
+                in1=gn_sb[:].unsqueeze(1).broadcast_to([P, NQ // T, E]),
+                op0=ALU.add,
+                op1=ALU.mult,
+            )
+
+        def finish(h, c0, c1):
+            m0, m1 = c0 // T, c1 // T
+            res = keep.tile([P, m1 - m0, E], F32, name="res%d_%d" % (h, c0))
+            for m in range(m0, m1):
+                nc.vector.scalar_tensor_tensor(
+                    out=res[:, m - m0, :],
+                    in0=y_ps[h][:, m * E : (m + 1) * E],
+                    scalar=rstd[PACK * h + m],
+                    in1=gate[h][:, m, :],
+                    op0=ALU.mult,
+                    op1=ALU.mult,
+                )
+            deal = DEAL[h]
+            rows = out[h].rearrange("(u s i) e -> s u i e", s=P, i=deal)
+            if deal == 1:
+                rows = rows[:, m0:m1, 0, :]
+            else:
+                rows = rows[:, m0 // deal, m0 % deal : m0 % deal + m1 - m0, :]
+            nc.sync.dma_start(out=rows, in_=res[:])
+
+        def start():
+            nc.gpsimd.memset(warm[:], 0.0)
+            nc.scalar.activation(out=warm[:, 1:2], in_=warm[:, 0:1], func=ACT.Silu)
+            nc.gpsimd.memset(k_mx[0][:, N:], 0)
+            nc.gpsimd.dma_start(out=kb_sb[:], in_=kb.rearrange("(p j) o -> p (j o)", j=PACK))
+            nc.gpsimd.dma_start(out=t_sb[:], in_=t.rearrange("(p j) o -> p (j o)", j=PACK))
+
+        load_k(0, 256)
+        start()
+        load_k(256, 384)
+        load_k(384, 512)
+        load_q(0, 0, 128)
+        load_q(0, 128, 256)
+        load_q(0, 256, 512)
+        load_q(1, 0, 256)
+        round_k(0, 256, "vector")
+        round_k(256, 384, "vector")
+        round_k(384, 512, "vector")
+        quantize_k(0)
+        quantize_k(1)
+        round_q(0, 0, "vector")
+        quantize_k(2)
+        quantize_k(3)
+        quantize_q(0, 0)
+        round_q(0, 128, "scalar")
+        move_k()
+        load_q(1, 256, 512)
+        load_v()
+        load_og(0)
+        load_og(1)
+        load_gn()
+        load_og(2)
+        load_og(3)
+        scores(0, 0, 128, 0)
+        quantize_q(0, 128)
+        silu(0, 0, 128, 0)
+        round_q(0, 256, "vector")
+        scores(0, 128, 256, 0)
+        silu(0, 128, 256, 0)
+        weigh(0, 0, 128)
+        quantize_q(0, 256)
+        round_q(1, 0, "scalar")
+        scores(0, 256, 512, 0)
+        silu(0, 256, 512, 0)
+        scores(0, 256, 512, 2)
+        silu(0, 256, 512, 2)
+        weigh(0, 128, 256)
+        scores(1, 0, 256, 0)
+        silu(1, 0, 256, 0)
+        scores(1, 0, 256, 2)
+        silu(1, 0, 256, 2)
+        quantize_q(1, 0)
+        quantize_w(0, 0, 128)
+        quantize_w(0, 128, 256)
+        weigh(0, 256, 512)
+        scores(1, 256, 512, 0)
+        silu(1, 256, 512, 0)
+        scores(1, 256, 512, 2)
+        silu(1, 256, 512, 2)
+        round_q(1, 256, "vector")
+        scores(2, 0, 256, 0)
+        silu(2, 0, 256, 0)
+        scores(2, 0, 256, 2)
+        silu(2, 0, 256, 2)
+        weigh(1, 0, 256)
+        quantize_q(1, 256)
+        round_v("vector")
+        scores(3, 0, 256, 0)
+        silu(3, 0, 256, 0)
+        scores(3, 0, 256, 2)
+        silu(3, 0, 256, 2)
+        quantize_w(0, 256, 512)
+        weigh(1, 256, 512)
+        quantize_v()
+        gate_tanh(0)
+        scores(2, 256, 512, 0)
+        silu(2, 256, 512, 0)
+        scores(2, 256, 512, 2)
+        silu(2, 256, 512, 2)
+        quantize_w(1, 0, 256)
+        weigh(2, 0, 256)
+        gate_tanh(1)
+        scores(3, 256, 512, 0)
+        silu(3, 256, 512, 0)
+        scores(3, 256, 512, 2)
+        silu(3, 256, 512, 2)
+        values(0, 0, 128)
+        values(0, 128, 256)
+        values(0, 256, 512)
+        values(1, 0, 256)
+        quantize_w(1, 256, 512)
+        values(1, 256, 512)
+        weigh(3, 0, 256)
+        gate_tanh(2)
+        gate_tanh(3)
+        quantize_w(2, 0, 256)
+        values(2, 0, 256)
+        weigh(2, 256, 512)
+        square(0, 0)
+        square(0, 1)
+        square(0, 2)
+        square(0, 3)
+        inv_rms(0, 4)
+        quantize_w(3, 0, 256)
+        values(3, 0, 256)
+        weigh(3, 256, 512)
+        square(1, 0)
+        square(1, 1)
+        square(1, 2)
+        square(1, 3)
+        inv_rms(4, 8)
+        quantize_w(2, 256, 512)
+        values(2, 256, 512)
+        gate_gain(0)
+        quantize_w(3, 256, 512)
+        values(3, 256, 512)
+        square(2, 0)
+        square(2, 1)
+        square(2, 2)
+        square(2, 3)
+        inv_rms(8, 12)
+        gate_gain(1)
+        finish(0, 0, 256)
+        finish(0, 256, 512)
+        square(3, 0)
+        square(3, 1)
+        square(3, 2)
+        square(3, 3)
+        inv_rms(12, 16)
+        gate_gain(2)
+        finish(1, 0, 256)
+        finish(1, 256, 512)
+        gate_gain(3)
+        finish(2, 0, 256)
+        finish(2, 256, 512)
+        finish(3, 0, 256)
+        finish(3, 256, 512)

@@ -18,7 +18,7 @@ P = 128
 R = 64
 PACK = 4
 T = 128
-RUN = 4
+RUN = 2
 BANK = 512
 DEAL = (1, 2, 2, 2)
 
@@ -81,11 +81,12 @@ def tile_rows_a_silu_kb_onorm_gate_kernel(tc, qT, kT, t, v, kb, gn, og, out):
                 nc.scalar.copy(out=dst, in_=src)
 
         def round_k(c0, c1, engine):
-            copy_on(
-                engine,
-                k_bf[:, :, c0 // PACK : c1 // PACK, :].rearrange("p r s j -> p s j r"),
-                k_raw[c0][:].rearrange("p j (s r) -> p s j r", r=PACK),
-            )
+            for r0 in range(0, PACK, RUN):
+                copy_on(
+                    engine,
+                    k_bf[:, r0 : r0 + RUN, c0 // PACK : c1 // PACK, :].rearrange("p r s j -> p s j r"),
+                    k_raw[c0][:].rearrange("p j (s r) -> p s j r", r=PACK)[:, :, :, r0 : r0 + RUN],
+                )
 
         def k_operand(g, r):
             rows = slice(R * g, R * (g + 1))
@@ -249,10 +250,10 @@ def tile_rows_a_silu_kb_onorm_gate_kernel(tc, qT, kT, t, v, kb, gn, og, out):
 
         def start():
             nc.gpsimd.memset(warm[:], 0.0)
+            nc.scalar.dma_start(out=kb_sb[:], in_=kb.rearrange("(p j) o -> p (j o)", j=PACK))
+            nc.scalar.dma_start(out=t_sb[:], in_=t.rearrange("(p j) o -> p (j o)", j=PACK))
             nc.scalar.activation(out=warm[:, 1:2], in_=warm[:, 0:1], func=ACT.Silu)
             nc.gpsimd.memset(k_mx[0][:, N:], 0)
-            nc.gpsimd.dma_start(out=kb_sb[:], in_=kb.rearrange("(p j) o -> p (j o)", j=PACK))
-            nc.gpsimd.dma_start(out=t_sb[:], in_=t.rearrange("(p j) o -> p (j o)", j=PACK))
 
         load_k(0, 256)
         start()

@@ -20,7 +20,8 @@ PACK = 4
 T = 128
 RUN = 2
 BANK = 512
-DEAL = (1, 2, 2, 2)
+DEAL = (1, 1, 1, 1)
+PIECE = 256
 
 
 def tile_rows_a_silu_kb_onorm_gate_kernel(tc, qT, kT, t, v, kb, gn, og, out):
@@ -41,7 +42,7 @@ def tile_rows_a_silu_kb_onorm_gate_kernel(tc, qT, kT, t, v, kb, gn, og, out):
         v_codes = keep.tile([P, E], U32, name="v_codes", align_bytes=64)
         v_scales = keep.tile([P, E], U8, name="v_scales", align_bytes=64)
         k_bf = keep.tile([R, PACK, T, PACK], BF16, name="k_bf", align_bytes=64)
-        k_mx = [keep.tile([P, N + N // 4], U32, name="k_mx%d" % g, align_bytes=64) for g in range(2)]
+        k_mx = [keep.tile([P, PACK, T + T // 4], U32, name="k_mx%d" % g, align_bytes=64) for g in range(2)]
         warm = keep.tile([P, 2], F32, name="warm")
         sumsq = keep.tile([P, H * PACK], F32, name="sumsq")
         squares = keep.tile([P, H * PACK, E], F32, name="squares")
@@ -90,16 +91,17 @@ def tile_rows_a_silu_kb_onorm_gate_kernel(tc, qT, kT, t, v, kb, gn, og, out):
 
         def k_operand(g, r):
             rows = slice(R * g, R * (g + 1))
-            codes = k_mx[g][rows, T * r : T * (r + 1)].bitcast(FP8X4)
-            scales = k_mx[g][rows, N:].bitcast(U8)[:, T * r : T * (r + 1)]
+            codes = k_mx[g][rows, r, 0:T].bitcast(FP8X4)
+            scales = k_mx[g][rows, r, T:].bitcast(U8)
             return codes, scales
 
         def quantize_k(r):
             codes, scales = k_operand(0, r)
             nc.vector.quantize_mx(out=codes, scales=scales, in_=k_bf[:, r, :, :].rearrange("p s j -> p (s j)"))
 
-        def move_k():
-            nc.sync.dma_start(out=k_mx[1][R:P, :].bitcast(I32), in_=k_mx[0][0:R, :].bitcast(I32))
+        def move_k(r0):
+            slots = slice(r0, r0 + 2)
+            nc.sync.dma_start(out=k_mx[1][R:P, slots, :].bitcast(I32), in_=k_mx[0][0:R, slots, :].bitcast(I32))
 
         def interleave(engine, dst, src):
             copy_on(
@@ -131,46 +133,58 @@ def tile_rows_a_silu_kb_onorm_gate_kernel(tc, qT, kT, t, v, kb, gn, og, out):
                 out=v_codes[:].bitcast(FP8X4), scales=v_scales[:], in_=v_bf[:].rearrange("p e j -> p (e j)")
             )
 
-        def scores(h, c0, c1, r0):
+        def score_passes(h, c0, c1, r0):
             width = c1 - c0
             g = h % 2
             rows = slice(R * g, R * (g + 1))
             bank = psum.tile([P, BANK], F32, name="s%d" % g, tag="s%d" % g)
             banks[h, c0, r0] = bank
+            passes = []
             for r in range(r0, r0 + BANK // width):
-                k_codes, k_scales = k_operand(g, r)
                 for b in range(0, width, T):
                     codes, scales, at = q_mx[h // 2, c0 + b]
                     col = (r - r0) * width + b
-                    nc.tensor.matmul_mx(
-                        out=bank[:, col : col + T],
-                        lhsT=k_codes,
-                        lhsT_scale=k_scales,
-                        rhs=codes[rows, at : at + T].bitcast(FP8X4),
-                        rhs_scale=scales[rows, at : at + T],
-                        start=True,
-                        stop=True,
-                    )
+                    passes.append((bank[:, col : col + T], k_operand(g, r), codes[rows, at : at + T], scales[rows, at : at + T]))
+            return passes
+
+        def score_pass(dst, keys, codes, scales):
+            nc.tensor.matmul_mx(
+                out=dst, lhsT=keys[0], lhsT_scale=keys[1], rhs=codes.bitcast(FP8X4), rhs_scale=scales, start=True, stop=True
+            )
+
+        def scores(h, c0, c1, r0):
+            for one in score_passes(h, c0, c1, r0):
+                score_pass(*one)
+
+        def pair(first, second):
+            for one, other in zip(score_passes(*first), score_passes(*second)):
+                score_pass(*one)
+                score_pass(*other)
 
         def silu(h, c0, c1, r0):
             width = c1 - c0
             if r0 == 0:
-                probs[h, c0] = keep.tile([P, PACK, width], F32, name="probs%d_%d" % (h, c0))
+                p_sb = keep.tile([P, PACK, width], F32, name="probs%d_%d" % (h, c0))
+                for b in range(0, width, T):
+                    probs[h, c0 + b] = (p_sb, b)
             for r in range(r0, r0 + BANK // width):
                 col = (r - r0) * width
                 nc.scalar.activation(
-                    out=probs[h, c0][:, r, :].rearrange("p (i s) -> p i s", i=DEAL[h]),
-                    in_=banks[h, c0, r0][:, col : col + width].rearrange("p (s i) -> p i s", i=DEAL[h]),
+                    out=probs[h, c0][0][:, r, :],
+                    in_=banks[h, c0, r0][:, col : col + width],
                     func=ACT.Silu,
                     bias=kb_sb[:, r : r + 1],
                 )
 
         def weigh(h, c0, c1):
             width = c1 - c0
-            w_bf[h, c0] = keep.tile([P, width, PACK], BF16, name="w%d_%d" % (h, c0), align_bytes=64)
+            first = c0 - c0 % PIECE
+            if c0 == first:
+                w_bf[h, c0] = keep.tile([P, PIECE, PACK], BF16, name="w%d_%d" % (h, c0), align_bytes=64)
+            p_sb, at = probs[h, c0]
             nc.vector.tensor_tensor(
-                out=w_bf[h, c0][:].rearrange("p (c i) r -> p c r i", i=RUN),
-                in0=probs[h, c0][:].rearrange("p r (c i) -> p c r i", i=RUN),
+                out=w_bf[h, first][:, c0 - first : c1 - first, :].rearrange("p (c i) r -> p c r i", i=RUN),
+                in0=p_sb[:, :, at : at + width].rearrange("p r (c i) -> p c r i", i=RUN),
                 in1=t_sb[:].unsqueeze(1).unsqueeze(3).broadcast_to([P, width // RUN, PACK, RUN]),
                 op=ALU.mult,
             )
@@ -253,7 +267,7 @@ def tile_rows_a_silu_kb_onorm_gate_kernel(tc, qT, kT, t, v, kb, gn, og, out):
             nc.scalar.dma_start(out=kb_sb[:], in_=kb.rearrange("(p j) o -> p (j o)", j=PACK))
             nc.scalar.dma_start(out=t_sb[:], in_=t.rearrange("(p j) o -> p (j o)", j=PACK))
             nc.scalar.activation(out=warm[:, 1:2], in_=warm[:, 0:1], func=ACT.Silu)
-            nc.gpsimd.memset(k_mx[0][:, N:], 0)
+            nc.gpsimd.memset(k_mx[0][:, :, T:], 0)
 
         load_k(0, 256)
         start()
@@ -262,125 +276,118 @@ def tile_rows_a_silu_kb_onorm_gate_kernel(tc, qT, kT, t, v, kb, gn, og, out):
         load_q(0, 0, 128)
         load_q(0, 128, 256)
         load_q(0, 256, 512)
-        load_q(1, 0, 256)
         round_k(0, 256, "vector")
         round_k(256, 384, "vector")
         round_k(384, 512, "vector")
+        round_q(0, 0, "scalar")
         quantize_k(0)
         quantize_k(1)
-        round_q(0, 0, "vector")
         quantize_k(2)
         quantize_k(3)
-        quantize_q(0, 0)
-        round_q(0, 128, "scalar")
-        move_k()
+        move_k(0)
+        move_k(2)
+        load_q(1, 0, 256)
         load_q(1, 256, 512)
         load_v()
         load_og(0)
-        load_og(1)
         load_gn()
+        load_og(1)
         load_og(2)
         load_og(3)
+        quantize_q(0, 0)
         scores(0, 0, 128, 0)
+        round_q(0, 128, "scalar")
         quantize_q(0, 128)
-        silu(0, 0, 128, 0)
-        round_q(0, 256, "vector")
         scores(0, 128, 256, 0)
-        silu(0, 128, 256, 0)
-        weigh(0, 0, 128)
+        round_q(0, 256, "vector")
+        silu(0, 0, 128, 0)
         quantize_q(0, 256)
-        round_q(1, 0, "scalar")
-        scores(0, 256, 512, 0)
-        silu(0, 256, 512, 0)
-        scores(0, 256, 512, 2)
-        silu(0, 256, 512, 2)
+        pair((0, 256, 512, 0), (1, 0, 256, 0))
+        weigh(0, 0, 128)
+        silu(0, 128, 256, 0)
+        pair((0, 256, 512, 2), (1, 0, 256, 2))
         weigh(0, 128, 256)
-        scores(1, 0, 256, 0)
+        round_q(1, 0, "vector")
+        silu(0, 256, 512, 0)
         silu(1, 0, 256, 0)
-        scores(1, 0, 256, 2)
-        silu(1, 0, 256, 2)
         quantize_q(1, 0)
-        quantize_w(0, 0, 128)
-        quantize_w(0, 128, 256)
-        weigh(0, 256, 512)
-        scores(1, 256, 512, 0)
-        silu(1, 256, 512, 0)
-        scores(1, 256, 512, 2)
-        silu(1, 256, 512, 2)
+        pair((2, 0, 256, 0), (1, 256, 512, 0))
+        silu(0, 256, 512, 2)
+        silu(1, 0, 256, 2)
+        pair((2, 0, 256, 2), (1, 256, 512, 2))
         round_q(1, 256, "vector")
-        scores(2, 0, 256, 0)
-        silu(2, 0, 256, 0)
-        scores(2, 0, 256, 2)
-        silu(2, 0, 256, 2)
-        weigh(1, 0, 256)
+        quantize_w(0, 0, 256)
         quantize_q(1, 256)
-        round_v("vector")
-        scores(3, 0, 256, 0)
-        silu(3, 0, 256, 0)
-        scores(3, 0, 256, 2)
-        silu(3, 0, 256, 2)
+        weigh(0, 256, 512)
+        silu(1, 256, 512, 0)
+        silu(2, 0, 256, 0)
+        pair((2, 256, 512, 0), (3, 0, 256, 0))
+        weigh(1, 0, 256)
         quantize_w(0, 256, 512)
+        round_v("vector")
+        silu(1, 256, 512, 2)
+        silu(2, 0, 256, 2)
+        pair((2, 256, 512, 2), (3, 0, 256, 2))
+        quantize_w(1, 0, 256)
         weigh(1, 256, 512)
         quantize_v()
-        gate_tanh(0)
-        scores(2, 256, 512, 0)
         silu(2, 256, 512, 0)
-        scores(2, 256, 512, 2)
-        silu(2, 256, 512, 2)
-        quantize_w(1, 0, 256)
-        weigh(2, 0, 256)
-        gate_tanh(1)
+        silu(3, 0, 256, 0)
         scores(3, 256, 512, 0)
-        silu(3, 256, 512, 0)
+        weigh(2, 0, 256)
+        gate_tanh(0)
+        silu(2, 256, 512, 2)
+        silu(3, 0, 256, 2)
         scores(3, 256, 512, 2)
-        silu(3, 256, 512, 2)
-        values(0, 0, 128)
-        values(0, 128, 256)
+        quantize_w(1, 256, 512)
+        values(0, 0, 256)
         values(0, 256, 512)
         values(1, 0, 256)
-        quantize_w(1, 256, 512)
         values(1, 256, 512)
-        weigh(3, 0, 256)
+        gate_tanh(1)
+        silu(3, 256, 512, 0)
         gate_tanh(2)
+        silu(3, 256, 512, 2)
         gate_tanh(3)
+        weigh(2, 256, 512)
         quantize_w(2, 0, 256)
         values(2, 0, 256)
-        weigh(2, 256, 512)
+        weigh(3, 0, 256)
         square(0, 0)
         square(0, 1)
         square(0, 2)
         square(0, 3)
         inv_rms(0, 4)
-        quantize_w(3, 0, 256)
-        values(3, 0, 256)
-        weigh(3, 256, 512)
         square(1, 0)
+        quantize_w(2, 256, 512)
+        values(2, 256, 512)
+        weigh(3, 256, 512)
         square(1, 1)
         square(1, 2)
         square(1, 3)
+        square(2, 0)
         inv_rms(4, 8)
-        quantize_w(2, 256, 512)
-        values(2, 256, 512)
+        quantize_w(3, 0, 256)
+        values(3, 0, 256)
         gate_gain(0)
         quantize_w(3, 256, 512)
         values(3, 256, 512)
-        square(2, 0)
+        gate_gain(1)
+        gate_gain(2)
         square(2, 1)
         square(2, 2)
         square(2, 3)
+        square(3, 0)
         inv_rms(8, 12)
-        gate_gain(1)
         finish(0, 0, 256)
         finish(0, 256, 512)
-        square(3, 0)
         square(3, 1)
         square(3, 2)
         square(3, 3)
         inv_rms(12, 16)
-        gate_gain(2)
         finish(1, 0, 256)
-        finish(1, 256, 512)
         gate_gain(3)
+        finish(1, 256, 512)
         finish(2, 0, 256)
         finish(2, 256, 512)
         finish(3, 0, 256)

from contextlib import ExitStack

import concourse.mybir as mybir

H, D, NQ, N, E = 4, 256, 512, 512, 128
FLOPS = 2 * H * N * NQ * (D + E)

F32 = mybir.dt.float32
BF16 = mybir.dt.bfloat16
U32 = mybir.dt.uint32
I32 = mybir.dt.int32
U8 = mybir.dt.uint8
FP8X4 = mybir.dt.float8_e4m3fn_x4
ACT = mybir.ActivationFunctionType
ALU = mybir.AluOpType

P = 128
R = 64
PACK = 4
T = 128
RUN = 2
BANK = 512
DEAL = (1, 1, 1, 1)
PIECE = 256


def tile_rows_a_silu_kb_onorm_gate_kernel(tc, qT, kT, t, v, kb, gn, og, out):
    nc = tc.nc
    with ExitStack() as ctx:
        keep = ctx.enter_context(tc.tile_pool(name="keep", bufs=1))
        psum = ctx.enter_context(tc.psum_pool(name="psum", bufs=2))
        ctx.enter_context(tc.manual_schedule())

        q_rows = qT.rearrange("h d n -> (h d) n")
        k_rows = kT[0].rearrange("(p j) n -> p j n", j=PACK)

        kb_sb = keep.tile([P, PACK], F32, name="kb_sb")
        t_sb = keep.tile([P, PACK], F32, name="t_sb")
        gn_sb = keep.tile([P, E], F32, name="gn_sb")
        v_raw = keep.tile([P, PACK, E], F32, name="v_raw")
        v_bf = keep.tile([P, E, PACK], BF16, name="v_bf", align_bytes=64)
        v_codes = keep.tile([P, E], U32, name="v_codes", align_bytes=64)
        v_scales = keep.tile([P, E], U8, name="v_scales", align_bytes=64)
        k_bf = keep.tile([R, PACK, T, PACK], BF16, name="k_bf", align_bytes=64)
        k_mx = [keep.tile([P, PACK, T + T // 4], U32, name="k_mx%d" % g, align_bytes=64) for g in range(2)]
        warm = keep.tile([P, 2], F32, name="warm")
        sumsq = keep.tile([P, H * PACK], F32, name="sumsq")
        squares = keep.tile([P, H * PACK, E], F32, name="squares")
        y_ps = [psum.tile([P, BANK], F32, name="y%d" % h, bufs=1) for h in range(H)]

        k_raw, q_raw, q_bf, q_mx, og_sb, gate = {}, {}, {}, {}, {}, {}
        banks, probs, w_bf, w_mx, rstd = {}, {}, {}, {}, {}

        def by_tile(rows, h):
            deal = DEAL[h]
            return rows.rearrange("(u s i) e -> s u (i e)", s=P, i=deal)


        def load_k(c0, c1):
            k_raw[c0] = keep.tile([R, PACK, c1 - c0], F32, name="k_raw%d" % c0)
            nc.sync.dma_start(out=k_raw[c0][:], in_=k_rows[:, :, c0:c1])

        def load_q(pair, c0, c1, queue=nc.sync):
            q_raw[pair, c0] = keep.tile([P, PACK, c1 - c0], F32, name="q_raw%d_%d" % (pair, c0))
            rows = q_rows[2 * D * pair : 2 * D * (pair + 1), :].rearrange("(p j) n -> p j n", j=PACK)
            queue.dma_start(out=q_raw[pair, c0][:], in_=rows[:, :, c0:c1])

        def load_v():
            nc.sync.dma_start(out=v_raw[:], in_=v[0].rearrange("(p j) e -> p j e", j=PACK))

        def load_gn():
            nc.sync.dma_start(out=gn_sb[:], in_=gn)

        def load_og(h):
            og_sb[h] = keep.tile([P, NQ // T, E], F32, name="og%d" % h)
            nc.sync.dma_start(out=og_sb[h][:].rearrange("p (u i) e -> p u (i e)", i=DEAL[h]), in_=by_tile(og[h], h))

        def copy_on(engine, dst, src):
            if engine == "vector":
                nc.vector.tensor_copy(out=dst, in_=src)
            else:
                nc.scalar.copy(out=dst, in_=src)

        def round_k(c0, c1, engine):
            for r0 in range(0, PACK, RUN):
                copy_on(
                    engine,
                    k_bf[:, r0 : r0 + RUN, c0 // PACK : c1 // PACK, :].rearrange("p r s j -> p s j r"),
                    k_raw[c0][:].rearrange("p j (s r) -> p s j r", r=PACK)[:, :, :, r0 : r0 + RUN],
                )

        def k_operand(g, r):
            rows = slice(R * g, R * (g + 1))
            codes = k_mx[g][rows, r, 0:T].bitcast(FP8X4)
            scales = k_mx[g][rows, r, T:].bitcast(U8)
            return codes, scales

        def quantize_k(r):
            codes, scales = k_operand(0, r)
            nc.vector.quantize_mx(out=codes, scales=scales, in_=k_bf[:, r, :, :].rearrange("p s j -> p (s j)"))

        def move_k(r0):
            slots = slice(r0, r0 + 2)
            nc.sync.dma_start(out=k_mx[1][R:P, slots, :].bitcast(I32), in_=k_mx[0][0:R, slots, :].bitcast(I32))

        def interleave(engine, dst, src):
            copy_on(
                engine,
                dst.rearrange("p (c i) j -> p c j i", i=RUN),
                src.rearrange("p j (c i) -> p c j i", i=RUN),
            )

        def round_q(pair, c0, engine):
            width = q_raw[pair, c0].shape[2]
            q_bf[pair, c0] = keep.tile([P, width, PACK], BF16, name="q_bf%d_%d" % (pair, c0), align_bytes=64)
            interleave(engine, q_bf[pair, c0][:], q_raw[pair, c0][:])

        def quantize_q(pair, c0):
            width = q_raw[pair, c0].shape[2]
            codes = keep.tile([P, width], U32, name="q_codes%d_%d" % (pair, c0), align_bytes=64)
            scales = keep.tile([P, width], U8, name="q_scales%d_%d" % (pair, c0), align_bytes=64)
            nc.vector.quantize_mx(
                out=codes[:].bitcast(FP8X4), scales=scales[:], in_=q_bf[pair, c0][:].rearrange("p n j -> p (n j)")
            )
            for b in range(0, width, T):
                q_mx[pair, c0 + b] = (codes, scales, b)

        def round_v(engine):
            interleave(engine, v_bf[:], v_raw[:])

        def quantize_v():
            nc.vector.quantize_mx(
                out=v_codes[:].bitcast(FP8X4), scales=v_scales[:], in_=v_bf[:].rearrange("p e j -> p (e j)")
            )

        def score_passes(h, c0, c1, r0):
            width = c1 - c0
            g = h % 2
            rows = slice(R * g, R * (g + 1))
            bank = psum.tile([P, BANK], F32, name="s%d" % g, tag="s%d" % g)
            banks[h, c0, r0] = bank
            passes = []
            for r in range(r0, r0 + BANK // width):
                for b in range(0, width, T):
                    codes, scales, at = q_mx[h // 2, c0 + b]
                    col = (r - r0) * width + b
                    passes.append((bank[:, col : col + T], k_operand(g, r), codes[rows, at : at + T], scales[rows, at : at + T]))
            return passes

        def score_pass(dst, keys, codes, scales):
            nc.tensor.matmul_mx(
                out=dst, lhsT=keys[0], lhsT_scale=keys[1], rhs=codes.bitcast(FP8X4), rhs_scale=scales, start=True, stop=True
            )

        def scores(h, c0, c1, r0):
            for one in score_passes(h, c0, c1, r0):
                score_pass(*one)

        def pair(first, second):
            for one, other in zip(score_passes(*first), score_passes(*second)):
                score_pass(*one)
                score_pass(*other)

        def silu(h, c0, c1, r0):
            width = c1 - c0
            if r0 == 0:
                p_sb = keep.tile([P, PACK, width], F32, name="probs%d_%d" % (h, c0))
                for b in range(0, width, T):
                    probs[h, c0 + b] = (p_sb, b)
            for r in range(r0, r0 + BANK // width):
                col = (r - r0) * width
                nc.scalar.activation(
                    out=probs[h, c0][0][:, r, :],
                    in_=banks[h, c0, r0][:, col : col + width],
                    func=ACT.Silu,
                    bias=kb_sb[:, r : r + 1],
                )

        def weigh(h, c0, c1):
            width = c1 - c0
            first = c0 - c0 % PIECE
            if c0 == first:
                w_bf[h, c0] = keep.tile([P, PIECE, PACK], BF16, name="w%d_%d" % (h, c0), align_bytes=64)
            p_sb, at = probs[h, c0]
            nc.vector.tensor_tensor(
                out=w_bf[h, first][:, c0 - first : c1 - first, :].rearrange("p (c i) r -> p c r i", i=RUN),
                in0=p_sb[:, :, at : at + width].rearrange("p r (c i) -> p c r i", i=RUN),
                in1=t_sb[:].unsqueeze(1).unsqueeze(3).broadcast_to([P, width // RUN, PACK, RUN]),
                op=ALU.mult,
            )

        def quantize_w(h, c0, c1):
            width = c1 - c0
            codes = keep.tile([P, width], U32, name="w_codes%d_%d" % (h, c0), align_bytes=64)
            scales = keep.tile([P, width], U8, name="w_scales%d_%d" % (h, c0), align_bytes=64)
            nc.vector.quantize_mx(
                out=codes[:].bitcast(FP8X4), scales=scales[:], in_=w_bf[h, c0][:].rearrange("p n r -> p (n r)")
            )
            w_mx[h, c0] = (codes, scales)

        def values(h, c0, c1):
            codes, scales = w_mx[h, c0]
            for b in range(0, c1 - c0, T):
                nc.tensor.matmul_mx(
                    out=y_ps[h][:, c0 + b : c0 + b + E],
                    lhsT=codes[:, b : b + T].bitcast(FP8X4),
                    lhsT_scale=scales[:, b : b + T],
                    rhs=v_codes[:].bitcast(FP8X4),
                    rhs_scale=v_scales[:],
                    start=True,
                    stop=True,
                )

        def square(h, m):
            col = PACK * h + m
            nc.scalar.activation(
                out=squares[:, col, :],
                in_=y_ps[h][:, m * E : (m + 1) * E],
                func=ACT.Square,
                accum_out=sumsq[:, col : col + 1],
            )

        def inv_rms(c0, c1):
            factor = keep.tile([P, c1 - c0], F32, name="factor%d" % c0)
            nc.scalar.activation(
                out=factor[:], in_=sumsq[:, c0:c1], func=ACT.Abs_reciprocal_sqrt, scale=1.0 / 32.0, bias=1024 * 1e-5
            )
            for c in range(c0, c1):
                rstd[c] = factor[:, c - c0 : c - c0 + 1]

        def gate_tanh(h):
            nc.scalar.activation(out=og_sb[h][:], in_=og_sb[h][:], func=ACT.Tanh, scale=0.5)

        def gate_gain(h):
            gate[h] = keep.tile([P, NQ // T, E], F32, name="gate%d" % h)
            nc.vector.scalar_tensor_tensor(
                out=gate[h][:],
                in0=og_sb[h][:],
                scalar=1.0,
                in1=gn_sb[:].unsqueeze(1).broadcast_to([P, NQ // T, E]),
                op0=ALU.add,
                op1=ALU.mult,
            )

        def finish(h, c0, c1):
            m0, m1 = c0 // T, c1 // T
            res = keep.tile([P, m1 - m0, E], F32, name="res%d_%d" % (h, c0))
            for m in range(m0, m1):
                nc.vector.scalar_tensor_tensor(
                    out=res[:, m - m0, :],
                    in0=y_ps[h][:, m * E : (m + 1) * E],
                    scalar=rstd[PACK * h + m],
                    in1=gate[h][:, m, :],
                    op0=ALU.mult,
                    op1=ALU.mult,
                )
            deal = DEAL[h]
            rows = out[h].rearrange("(u s i) e -> s u i e", s=P, i=deal)
            if deal == 1:
                rows = rows[:, m0:m1, 0, :]
            else:
                rows = rows[:, m0 // deal, m0 % deal : m0 % deal + m1 - m0, :]
            nc.sync.dma_start(out=rows, in_=res[:])

        def start():
            nc.gpsimd.memset(warm[:], 0.0)
            nc.scalar.dma_start(out=kb_sb[:], in_=kb.rearrange("(p j) o -> p (j o)", j=PACK))
            nc.scalar.dma_start(out=t_sb[:], in_=t.rearrange("(p j) o -> p (j o)", j=PACK))
            nc.scalar.activation(out=warm[:, 1:2], in_=warm[:, 0:1], func=ACT.Silu)
            nc.gpsimd.memset(k_mx[0][:, :, T:], 0)

        load_k(0, 256)
        start()
        load_k(256, 384)
        load_k(384, 512)
        load_q(0, 0, 128)
        load_q(0, 128, 256)
        load_q(0, 256, 512)
        round_k(0, 256, "vector")
        round_k(256, 384, "vector")
        round_k(384, 512, "vector")
        round_q(0, 0, "scalar")
        quantize_k(0)
        quantize_k(1)
        quantize_k(2)
        quantize_k(3)
        move_k(0)
        move_k(2)
        load_q(1, 0, 256)
        load_q(1, 256, 512)
        load_v()
        load_og(0)
        load_gn()
        load_og(1)
        load_og(2)
        load_og(3)
        quantize_q(0, 0)
        scores(0, 0, 128, 0)
        round_q(0, 128, "scalar")
        quantize_q(0, 128)
        scores(0, 128, 256, 0)
        round_q(0, 256, "vector")
        silu(0, 0, 128, 0)
        quantize_q(0, 256)
        pair((0, 256, 512, 0), (1, 0, 256, 0))
        weigh(0, 0, 128)
        silu(0, 128, 256, 0)
        pair((0, 256, 512, 2), (1, 0, 256, 2))
        weigh(0, 128, 256)
        round_q(1, 0, "vector")
        silu(0, 256, 512, 0)
        silu(1, 0, 256, 0)
        quantize_q(1, 0)
        pair((2, 0, 256, 0), (1, 256, 512, 0))
        silu(0, 256, 512, 2)
        silu(1, 0, 256, 2)
        pair((2, 0, 256, 2), (1, 256, 512, 2))
        round_q(1, 256, "vector")
        quantize_w(0, 0, 256)
        quantize_q(1, 256)
        weigh(0, 256, 512)
        silu(1, 256, 512, 0)
        silu(2, 0, 256, 0)
        pair((2, 256, 512, 0), (3, 0, 256, 0))
        weigh(1, 0, 256)
        quantize_w(0, 256, 512)
        round_v("vector")
        silu(1, 256, 512, 2)
        silu(2, 0, 256, 2)
        pair((2, 256, 512, 2), (3, 0, 256, 2))
        quantize_w(1, 0, 256)
        weigh(1, 256, 512)
        quantize_v()
        silu(2, 256, 512, 0)
        silu(3, 0, 256, 0)
        scores(3, 256, 512, 0)
        weigh(2, 0, 256)
        gate_tanh(0)
        silu(2, 256, 512, 2)
        silu(3, 0, 256, 2)
        scores(3, 256, 512, 2)
        quantize_w(1, 256, 512)
        values(0, 0, 256)
        values(0, 256, 512)
        values(1, 0, 256)
        values(1, 256, 512)
        gate_tanh(1)
        silu(3, 256, 512, 0)
        gate_tanh(2)
        silu(3, 256, 512, 2)
        gate_tanh(3)
        weigh(2, 256, 512)
        quantize_w(2, 0, 256)
        values(2, 0, 256)
        weigh(3, 0, 256)
        square(0, 0)
        square(0, 1)
        square(0, 2)
        square(0, 3)
        inv_rms(0, 4)
        square(1, 0)
        quantize_w(2, 256, 512)
        values(2, 256, 512)
        weigh(3, 256, 512)
        square(1, 1)
        square(1, 2)
        square(1, 3)
        square(2, 0)
        inv_rms(4, 8)
        quantize_w(3, 0, 256)
        values(3, 0, 256)
        gate_gain(0)
        quantize_w(3, 256, 512)
        values(3, 256, 512)
        gate_gain(1)
        gate_gain(2)
        square(2, 1)
        square(2, 2)
        square(2, 3)
        square(3, 0)
        inv_rms(8, 12)
        finish(0, 0, 256)
        finish(0, 256, 512)
        square(3, 1)
        square(3, 2)
        square(3, 3)
        inv_rms(12, 16)
        finish(1, 0, 256)
        gate_gain(3)
        finish(1, 256, 512)
        finish(2, 0, 256)
        finish(2, 256, 512)
        finish(3, 0, 256)
        finish(3, 256, 512)
